import numpy as np, ml_dtypes
CORES = [23,119,17,113]
N = 4
import mx_ref
BF = ml_dtypes.bfloat16
def rowtile(v, k):
    z = np.concatenate([v, np.zeros((1, v.shape[1]), BF)])
    return np.concatenate([np.ascontiguousarray(z[k[:, 4 * m:4 * m + 4]].transpose(0, 2, 1)).reshape(128, -1) for m in range(k.shape[1] // 4)], axis=1)
def cut(t, i, w=512):
    return t[:, w * i:w * i + w]
def f(rng, *shape):
    return mx_ref.flush((rng.standard_normal(shape, dtype=np.float32) * np.exp2(rng.integers(-2, 3, shape[:-1] + (1,)))).astype(BF))
def wide(rng, *shape, cols=0):
    v = rng.standard_normal(shape, dtype=np.float32) * np.exp2(rng.integers(-12, 13, shape)).astype(np.float32)
    if cols: v *= np.repeat(np.exp2(rng.integers(-cols, cols + 1, shape[:-2] + (1, shape[-1] // 4))) * (rng.random(shape[:-2] + (1, shape[-1] // 4)) > 0.0625), 4, axis=-1).astype(np.float32)
    return mx_ref.flush(v.astype(BF))
T, GW, CAPP = 1024, 1024, 256
def counts(rng):
    n = rng.integers(0, CAPP + 1, (N, N))
    for e in range(N):
        if n[:, e].sum() < CAPP: n[rng.integers(0, N), e] = CAPP
    return n
def lists(rng, n):
    l = np.full((N, N, 512), -1)
    for s in range(N):
        for e in range(N): l[s, e, :n[s, e]] = rng.integers(0, T, n[s, e])
    return l
def store(l):
    return np.ascontiguousarray(l.reshape(N, N, 128, 4).transpose(0, 2, 1, 3)).reshape(N, 128, 4 * N).astype(np.int32)
def setup_inputs(rng):
    return {"x": f(rng, N, T, 128), "dy": f(rng, N, T, GW), "pick": store(lists(rng, counts(rng)))}
def setup_inputs_alike(rng):
    d = setup_inputs(rng); l = np.full((N, N, 512), -1); n = rng.integers(CAPP // 2, CAPP + 1)
    l[:, :, :n] = rng.integers(0, T, n)
    d["pick"] = store(l); return d
def setup_inputs_counts(rng):
    d = setup_inputs(rng)
    n = np.array([0, 1, 33, CAPP])[(np.arange(N)[:, None] + np.arange(N) + rng.integers(0, 4)) % 4][rng.permutation(N)]
    d["pick"] = store(lists(rng, n)); return d
def setup_inputs_giant(rng):
    d = setup_inputs(rng); l = lists(rng, rng.integers(64, CAPP + 1, (N, N)))
    for s in range(N):
        k = rng.permutation(T); kx, kg = k[:T // 32], k[T // 32:T // 16]
        d["x"][s, kx] = (d["x"][s, kx].astype(np.float32) * np.float32(4096)).astype(BF)
        d["dy"][s, kg] = (d["dy"][s, kg].astype(np.float32) * np.float32(4096)).astype(BF)
        for e in range(N):
            i = rng.permutation(32)
            l[s, e, i[0]], l[s, e, i[1]] = rng.choice(kx), rng.choice(kg)
    d["pick"] = store(l); return d
def setup_inputs_reversed(rng):
    d = setup_inputs(rng); n = counts(rng); l = lists(rng, n)
    for s in range(N):
        for e in range(N): l[s, e, :n[s, e]] = np.sort(l[s, e, :n[s, e]])[::-1]
    d["pick"] = store(l); return d
def setup_inputs_spread(rng):
    d = setup_inputs(rng); d["x"] = wide(rng, N, T, 128); d["dy"] = wide(rng, N, T, GW)
    d["pick"] = store(lists(rng, rng.integers(CAPP // 2, CAPP + 1, (N, N)))); return d
def check_inputs(d):
    b = []
    for q in ("x", "dy"):
        v = np.abs(np.asarray(d[q]).astype(np.float32))
        if not np.isfinite(v).all() or ((v != 0) & ((v < 2.0 ** -30) | (v > 2.0 ** 30))).any(): b.append(q)
    for s in range(N):
        for e in range(N):
            k = np.asarray(d["pick"][s])[:, 4 * e:4 * e + 4].reshape(-1); n = int((k >= 0).sum())
            if n > CAPP or k.max() >= T or (k[:n] < 0).any() or (k[n:] != -1).any(): b.append("pick")
    return b
def reference(x, dy, pick):
    y = np.zeros((N, 128, GW), np.float32)
    for e in range(N):
        for s in range(N):
            k = pick[s][:, 4 * e:4 * e + 4]
            X, G = mx_ref.quantize(rowtile(x[s], k)), rowtile(dy[s], k)
            for i in range(GW // 512): y[e][:, 512 * i:512 * i + 512] += mx_ref.matmul(X, mx_ref.quantize(cut(G, i, 2048)))
    return {"y": y}

@@ -1,0 +1,207 @@
+from concourse.bass import DstId, RemoteDMATransfer, IndirectOffsetOnAxis
+from concourse.mybir import dt, ActivationFunctionType
+
+TOK, XW, GW = 1024, 128, 1024
+HALF = GW // 2
+QUADS = 64
+COLS = HALF + 2 * XW
+
+SCRATCH = {
+    "idx": ("sbuf", [128, 8], "int32"),
+    "ys": ("sbuf", [128, GW], "float32"),
+    "acc": ("psum", [128, GW], "float32"),
+}
+for _k in range(2):
+    SCRATCH["rd%d" % _k] = ("sbuf", [128, 4 * GW], "bfloat16")
+    SCRATCH["rx%d" % _k] = ("sbuf", [128, 4 * XW], "bfloat16")
+for _s in range(4):
+    SCRATCH["gt%d" % _s] = ("sbuf", [128, 4 * HALF], "bfloat16")
+    SCRATCH["xt%d" % _s] = ("sbuf", [128, 8 * XW], "bfloat16")
+    SCRATCH["oc%d" % _s] = ("sbuf", [128, COLS], "float8_e4m3fn_x4")
+    SCRATCH["op%d" % _s] = ("sbuf", [128, COLS], "uint8")
+    SCRATCH["ic%d" % _s] = ("sbuf", [128, COLS], "float8_e4m3fn_x4")
+    SCRATCH["ip%d" % _s] = ("sbuf", [128, COLS], "uint8")
+
+SEMAPHORES = ["m0a", "m0b", "m1", "sent", "mm0", "mm1", "ev0", "ev1", "st0", "st1"]
+for _k in range(2):
+    SEMAPHORES += ["idx%d" % _k, "zx%d" % _k]
+    SEMAPHORES += ["d%d_%d" % (_k, t) for t in range(4)] + ["x%d_%d" % (_k, t) for t in range(4)]
+    SEMAPHORES += ["sg%d" % _k, "sx%d" % _k, "vg%d" % _k, "vx%d" % _k]
+for _s in range(4):
+    SEMAPHORES += ["qg%d" % _s, "qx%d" % _s, "arr%d" % _s]
+
+
+def bits(mask_engines):
+    return sum(1 << e for e in mask_engines)
+
+
+def rank_program(g, core, T, topo):
+    r = T.rank_of(core)
+    if r is None:
+        return
+    cores = T.cores
+    n = len(cores)
+    sem = T.sem
+    off = [e for e in range(n) if topo.chip(cores[e]) != topo.chip(core)]
+    near = [e for e in range(n) if e != r and topo.chip(cores[e]) == topo.chip(core)][0]
+    slot = [off[0], off[1], near, r]
+
+    far_eng = topo.engines(core, cores[off[0]])
+    half = len(far_eng) // 2
+    far_mask = [bits(far_eng[:half]), bits(far_eng[half:])]
+    near_eng = [e for e in topo.engines(core, cores[near]) if e not in far_eng]
+    near_mask = bits(near_eng)
+
+    for k in range(2):
+        for h, q in ((0, g.sync), (1, g.scalar)):
+            e = slot[2 * k + h]
+            q.dma_start(T.idx[QUADS * h:QUADS * h + QUADS, 4 * k:4 * k + 4],
+                        T.pick[0:QUADS, 4 * e:4 * e + 4]).then_inc(sem["idx%d" % k], 16)
+
+    def gather(table, land, w, k, t, name):
+        g.indirect_dma_start(T[land][:, t * w:(t + 1) * w], None, T[table][:],
+                             IndirectOffsetOnAxis(ap=T.idx[:, 4 * k + t:4 * k + t + 1], axis=0),
+                             bounds_check=TOK - 1, oob_is_err=False).then_inc(sem[name], 16)
+
+    def dy(k, t):
+        gather("dy", "rd%d" % k, GW, k, t, "d%d_%d" % (k, t))
+
+    def x(k, t):
+        gather("x", "rx%d" % k, XW, k, t, "x%d_%d" % (k, t))
+
+    def dst_id(e):
+        rid, pid, _ = topo.addr(cores[e])
+        return DstId(rid=rid, pnc=pid)
+
+    sent = [0]
+
+    def send(slots, codes, a, b):
+        tr = []
+        for s in slots:
+            src, dst = ("oc%d" % s, "ic%d" % r) if codes else ("op%d" % s, "ip%d" % r)
+            src, dst = T[src][:, a:b], T[dst][:, a:b]
+            if codes:
+                src, dst = src.bitcast(dt.uint8), dst.bitcast(dt.uint8)
+            far = s < 2
+            sent[0] += half if far else len(near_eng)
+            tr.append(RemoteDMATransfer(dst_ids=[dst_id(slot[s])], dma_engine_mask=far_mask[s] if far else near_mask,
+                                        remote_sem=sem["arr%d" % r], src=src, dst=dst))
+        g.remote_dma_fused(tr, local_sem=sem.sent)
+
+    g.wait_ge(sem.idx0, 32)
+    g.wait_ge(sem.m0a, 1)
+    dy(0, 0)
+    g.wait_ge(sem.m0b, 2)
+    for t in (1, 2, 3):
+        dy(0, t)
+    for t in (0, 1, 2):
+        x(0, t)
+    g.wait_ge(sem.qg0, 1)
+    g.wait_ge(sem.qg1, 1)
+    send((0, 1), True, 0, HALF)
+    x(0, 3)
+    g.wait_ge(sem.idx1, 32)
+    g.wait_ge(sem.m1, 3)
+    for t in (0, 1, 2):
+        dy(1, t)
+    g.wait_ge(sem.qx0, 1)
+    g.wait_ge(sem.qx1, 1)
+    send((0, 1), True, HALF, COLS)
+    send((0, 1), False, 0, COLS)
+    dy(1, 3)
+    for t in (0, 1, 2, 3):
+        x(1, t)
+    g.wait_ge(sem.qg2, 1)
+    send((2,), True, 0, HALF)
+    send((2,), False, 0, HALF)
+    g.wait_ge(sem.qx2, 1)
+    send((2,), True, HALF, COLS)
+    send((2,), False, HALF, COLS)
+    g.wait_ge(sem.sent, sent[0])
+
+    v, a = g.vector, g.scalar
+
+    def views(kind, s, h, t):
+        lo = QUADS * (s % 2)
+        if kind == "g":
+            return (T["gt%d" % s][QUADS * h:QUADS * h + QUADS, t:4 * HALF:4],
+                    T["rd%d" % (s // 2)][lo:lo + QUADS, t * GW + h * HALF:t * GW + (h + 1) * HALF])
+        return (T["xt%d" % s][QUADS * h:QUADS * h + QUADS, 4 * XW * h + t:4 * XW * (h + 1):4],
+                T["rx%d" % (s // 2)][lo:lo + QUADS, t * XW:(t + 1) * XW])
+
+    def copies(kind, k, t):
+        name = ("d%d_%d" if kind == "g" else "x%d_%d") % (k, t)
+        v.wait_ge(sem[name], 16)
+        a.wait_ge(sem[name], 16)
+        o, i = views(kind, 2 * k + 1, 1, t)
+        a.activation(o, i, ActivationFunctionType.Copy).then_inc(sem["s%s%d" % (kind, k)], 1)
+        for s, h in ((2 * k, 0), (2 * k, 1), (2 * k + 1, 0)):
+            o, i = views(kind, s, h, t)
+            v.tensor_copy(o, i).then_inc(sem["v%s%d" % (kind, k)], 1)
+
+    def quant(kind, k):
+        v.wait_ge(sem["v%s%d" % (kind, k)], 12)
+        if kind == "x":
+            v.wait_ge(sem["zx%d" % k], 4)
+        for s in (2 * k, 2 * k + 1):
+            if s % 2:
+                v.wait_ge(sem["s%s%d" % (kind, k)], 4)
+            lo, hi = (0, HALF) if kind == "g" else (HALF, COLS)
+            tile = T["gt%d" % s] if kind == "g" else T["xt%d" % s]
+            v.quantize_mx(T["oc%d" % s][:, lo:hi], T["op%d" % s][:, lo:hi], tile[:]).then_inc(sem["q%s%d" % (kind, s)], 1)
+
+    def zeros_x(k):
+        for s in (2 * k, 2 * k + 1):
+            v.memset(T["xt%d" % s][QUADS:128, 0:4 * XW], 0.0).then_inc(sem["zx%d" % k], 1)
+            v.memset(T["xt%d" % s][0:QUADS, 4 * XW:8 * XW], 0.0).then_inc(sem["zx%d" % k], 1)
+
+    v.memset(T.rd0[:, 0:GW], 0.0).then_inc(sem.m0a, 1)
+    v.memset(T.rd0[:, GW:4 * GW], 0.0).then_inc(sem.m0b, 1)
+    v.memset(T.rx0[:], 0.0).then_inc(sem.m0b, 1)
+    zeros_x(0)
+    copies("g", 0, 0)
+    v.memset(T.rd1[:, 0:2 * GW], 0.0).then_inc(sem.m1, 1)
+    copies("g", 0, 1)
+    v.memset(T.rd1[:, 2 * GW:4 * GW], 0.0).then_inc(sem.m1, 1)
+    copies("g", 0, 2)
+    v.memset(T.rx1[:], 0.0).then_inc(sem.m1, 1)
+    copies("g", 0, 3)
+    quant("g", 0)
+    zeros_x(1)
+    for t in range(4):
+        copies("x", 0, t)
+    quant("x", 0)
+    for t in range(4):
+        copies("g", 1, t)
+    quant("g", 1)
+    for t in range(4):
+        copies("x", 1, t)
+    quant("x", 1)
+
+    pe = g.tensor
+    order = [off[0], off[1], r, near]
+    for j, s in enumerate(order):
+        if s == r:
+            pe.wait_ge(sem.qg3, 1)
+            pe.wait_ge(sem.qx3, 1)
+            c, p = T.oc3, T.op3
+        else:
+            pe.wait_ge(sem["arr%d" % s], 4 * len(near_eng) if s == near else 3 * half)
+            c, p = T["ic%d" % s], T["ip%d" % s]
+        for h in range(2):
+            w = slice(HALF + XW * h, HALF + XW * (h + 1))
+            m = pe.matmul_mx(T.acc[:, HALF * h:HALF * (h + 1)], c[:, w], p[:, w], c[:, 0:HALF], p[:, 0:HALF],
+                             j == 0, j == n - 1)
+            if j == n - 1:
+                m.then_inc(sem["mm%d" % h], 1)
+
+    v.wait_ge(sem.mm0, 1)
+    v.tensor_copy(T.ys[:, 0:HALF], T.acc[:, 0:HALF]).then_inc(sem.ev0, 1)
+    g.sync.wait_ge(sem.ev0, 1)
+    g.sync.dma_start(T.y[:, 0:HALF], T.ys[:, 0:HALF]).then_inc(sem.st0, 16)
+    g.sync.wait_ge(sem.st0, 16)
+    a.wait_ge(sem.mm1, 1)
+    a.activation(T.ys[:, HALF:GW], T.acc[:, HALF:GW], ActivationFunctionType.Copy).then_inc(sem.ev1, 1)
+    a.wait_ge(sem.ev1, 1)
+    a.dma_start(T.y[:, HALF:GW], T.ys[:, HALF:GW]).then_inc(sem.st1, 16)
+    a.wait_ge(sem.st1, 16)

@@ -2,18 +2,22 @@ from concourse.bass import DstId, RemoteDMATransfer, IndirectOffsetOnAxis
 from concourse.mybir import dt, ActivationFunctionType
 
 TOK, XW, GW = 1024, 128, 1024
+JW = XW + GW
 HALF = GW // 2
 QUADS = 64
 COLS = HALF + 2 * XW
 
 SCRATCH = {
-    "idx": ("sbuf", [128, 8], "int32"),
+    "tab": ("dram", [TOK, JW], "bfloat16"),
+    "idx": ("sbuf", [128, 16], "int32"),
+    "rx": ("sbuf", [128, 4 * XW], "bfloat16"),
+    "rd0": ("sbuf", [128, 2 * GW], "bfloat16"),
+    "rd1": ("sbuf", [128, 2 * GW], "bfloat16"),
+    "rj2": ("sbuf", [128, 2 * JW], "bfloat16"),
+    "rj3": ("sbuf", [128, 2 * JW], "bfloat16"),
     "ys": ("sbuf", [128, GW], "float32"),
     "acc": ("psum", [128, GW], "float32"),
 }
-for _k in range(2):
-    SCRATCH["rd%d" % _k] = ("sbuf", [128, 4 * GW], "bfloat16")
-    SCRATCH["rx%d" % _k] = ("sbuf", [128, 4 * XW], "bfloat16")
 for _s in range(4):
     SCRATCH["gt%d" % _s] = ("sbuf", [128, 4 * HALF], "bfloat16")
     SCRATCH["xt%d" % _s] = ("sbuf", [128, 8 * XW], "bfloat16")
@@ -22,17 +26,17 @@ for _s in range(4):
     SCRATCH["ic%d" % _s] = ("sbuf", [128, COLS], "float8_e4m3fn_x4")
     SCRATCH["ip%d" % _s] = ("sbuf", [128, COLS], "uint8")
 
-SEMAPHORES = ["m0a", "m0b", "m1", "sent", "mm0", "mm1", "ev0", "ev1", "st0", "st1"]
-for _k in range(2):
-    SEMAPHORES += ["idx%d" % _k, "zx%d" % _k]
-    SEMAPHORES += ["d%d_%d" % (_k, t) for t in range(4)] + ["x%d_%d" % (_k, t) for t in range(4)]
-    SEMAPHORES += ["sg%d" % _k, "sx%d" % _k, "vg%d" % _k, "vx%d" % _k]
+SEMAPHORES = ["idx", "tab", "ma", "mb", "mx", "m2", "m3", "sent", "mm0", "mm1", "ev0", "ev1", "st0", "st1"]
 for _s in range(4):
+    SEMAPHORES += ["g%d_0" % _s, "g%d_1" % _s, "zx%d" % _s]
+    SEMAPHORES += ["sg%d" % _s, "sx%d" % _s, "vg%d" % _s, "vx%d" % _s]
     SEMAPHORES += ["qg%d" % _s, "qx%d" % _s, "arr%d" % _s]
+for _s in range(2):
+    SEMAPHORES += ["x%d_0" % _s, "x%d_1" % _s]
 
 
-def bits(mask_engines):
-    return sum(1 << e for e in mask_engines)
+def bits(engines):
+    return sum(1 << e for e in engines)
 
 
 def rank_program(g, core, T, topo):
@@ -48,26 +52,40 @@ def rank_program(g, core, T, topo):
 
     far_eng = topo.engines(core, cores[off[0]])
     half = len(far_eng) // 2
-    far_mask = [bits(far_eng[:half]), bits(far_eng[half:])]
     near_eng = [e for e in topo.engines(core, cores[near]) if e not in far_eng]
-    near_mask = bits(near_eng)
 
-    for k in range(2):
-        for h, q in ((0, g.sync), (1, g.scalar)):
-            e = slot[2 * k + h]
-            q.dma_start(T.idx[QUADS * h:QUADS * h + QUADS, 4 * k:4 * k + 4],
-                        T.pick[0:QUADS, 4 * e:4 * e + 4]).then_inc(sem["idx%d" % k], 16)
+    g.sync.dma_start(T.idx[0:QUADS, 0:15], T.pick[0:QUADS, 0:15]).then_inc(sem.idx, 16)
+    g.scalar.dma_start(T.idx[QUADS:128, 0:15], T.pick[0:QUADS, 1:16]).then_inc(sem.idx, 16)
 
-    def gather(table, land, w, k, t, name):
-        g.indirect_dma_start(T[land][:, t * w:(t + 1) * w], None, T[table][:],
-                             IndirectOffsetOnAxis(ap=T.idx[:, 4 * k + t:4 * k + t + 1], axis=0),
-                             bounds_check=TOK - 1, oob_is_err=False).then_inc(sem[name], 16)
+    tabs = [0]
 
-    def dy(k, t):
-        gather("dy", "rd%d" % k, GW, k, t, "d%d_%d" % (k, t))
+    def tab(kind, lo, hi):
+        to, of = (T.tab[lo:hi, XW:JW], T.dy[lo:hi, :]) if kind == "g" else (T.tab[lo:hi, 0:XW], T.x[lo:hi, :])
+        g.sync.dma_start(to, of).then_inc(sem.tab, 16)
+        tabs[0] += 16
 
-    def x(k, t):
-        gather("x", "rx%d" % k, XW, k, t, "x%d_%d" % (k, t))
+    for j in range(3):
+        tab("g", 128 * j, 128 * j + 128)
+    g.sync.wait_ge(sem.g0_0, 16)
+    tab("g", 384, 512)
+    g.sync.wait_ge(sem.g0_1, 16)
+    tab("x", 0, 512)
+    g.sync.wait_ge(sem.g1_0, 16)
+    tab("x", 512, 1024)
+    g.sync.wait_ge(sem.g1_1, 16)
+    for j in range(4, 8):
+        tab("g", 128 * j, 128 * j + 128)
+
+    def gather(kind, s, u):
+        c = 4 * slot[s] + 2 * u
+        if kind == "x":
+            land, table = T.rx[:, (2 * s + u) * XW:(2 * s + u + 1) * XW], T.x[:]
+        elif s < 2:
+            land, table = T["rd%d" % s][:, u * GW:(u + 1) * GW], T.dy[:]
+        else:
+            land, table = T["rj%d" % s][:, u * JW:(u + 1) * JW], T.tab[:]
+        g.indirect_dma_start(land, None, table, IndirectOffsetOnAxis(ap=T.idx[:, c:c + 1], axis=0),
+                             bounds_check=TOK - 1, oob_is_err=False).then_inc(sem["%s%d_%d" % (kind, s, u)], 16)
 
     def dst_id(e):
         rid, pid, _ = topo.addr(cores[e])
@@ -75,118 +93,139 @@ def rank_program(g, core, T, topo):
 
     sent = [0]
 
-    def send(slots, codes, a, b):
+    def send(parts, codes, lo, hi):
         tr = []
-        for s in slots:
+        for s, engines in parts:
             src, dst = ("oc%d" % s, "ic%d" % r) if codes else ("op%d" % s, "ip%d" % r)
-            src, dst = T[src][:, a:b], T[dst][:, a:b]
+            src, dst = T[src][:, lo:hi], T[dst][:, lo:hi]
             if codes:
                 src, dst = src.bitcast(dt.uint8), dst.bitcast(dt.uint8)
-            far = s < 2
-            sent[0] += half if far else len(near_eng)
-            tr.append(RemoteDMATransfer(dst_ids=[dst_id(slot[s])], dma_engine_mask=far_mask[s] if far else near_mask,
+            sent[0] += len(engines)
+            tr.append(RemoteDMATransfer(dst_ids=[dst_id(slot[s])], dma_engine_mask=bits(engines),
                                         remote_sem=sem["arr%d" % r], src=src, dst=dst))
         g.remote_dma_fused(tr, local_sem=sem.sent)
 
-    g.wait_ge(sem.idx0, 32)
-    g.wait_ge(sem.m0a, 1)
-    dy(0, 0)
-    g.wait_ge(sem.m0b, 2)
-    for t in (1, 2, 3):
-        dy(0, t)
-    for t in (0, 1, 2):
-        x(0, t)
+    far = [(0, far_eng[:half]), (1, far_eng[half:])]
+    g.wait_ge(sem.idx, 32)
+    g.wait_ge(sem.ma, 1)
+    gather("g", 0, 0)
+    g.wait_ge(sem.mb, 2)
+    gather("g", 0, 1)
+    gather("g", 1, 0)
+    gather("g", 1, 1)
+    g.wait_ge(sem.mx, 1)
+    gather("x", 0, 0)
+    gather("x", 0, 1)
+    gather("x", 1, 0)
     g.wait_ge(sem.qg0, 1)
     g.wait_ge(sem.qg1, 1)
-    send((0, 1), True, 0, HALF)
-    x(0, 3)
-    g.wait_ge(sem.idx1, 32)
-    g.wait_ge(sem.m1, 3)
-    for t in (0, 1, 2):
-        dy(1, t)
+    send(far, True, 0, HALF)
+    gather("x", 1, 1)
+    g.wait_ge(sem.m2, 1)
+    g.wait_ge(sem.tab, tabs[0])
+    gather("g", 2, 0)
+    gather("g", 2, 1)
     g.wait_ge(sem.qx0, 1)
     g.wait_ge(sem.qx1, 1)
-    send((0, 1), True, HALF, COLS)
-    send((0, 1), False, 0, COLS)
-    dy(1, 3)
-    for t in (0, 1, 2, 3):
-        x(1, t)
-    g.wait_ge(sem.qg2, 1)
-    send((2,), True, 0, HALF)
-    send((2,), False, 0, HALF)
+    send(far, True, HALF, COLS)
+    send(far, False, 0, COLS)
+    g.wait_ge(sem.m3, 1)
+    gather("g", 3, 0)
+    gather("g", 3, 1)
     g.wait_ge(sem.qx2, 1)
-    send((2,), True, HALF, COLS)
-    send((2,), False, HALF, COLS)
+    g.wait_ge(sem.qg2, 1)
+    send([(2, near_eng)], True, 0, COLS)
+    send([(2, far_eng)], False, 0, COLS)
     g.wait_ge(sem.sent, sent[0])
 
     v, a = g.vector, g.scalar
 
-    def views(kind, s, h, t):
-        lo = QUADS * (s % 2)
+    def views(kind, s, u, i, h):
+        t = 2 * u + i
+        lo, to = slice(QUADS * i, QUADS * (i + 1)), slice(QUADS * h, QUADS * (h + 1))
         if kind == "g":
-            return (T["gt%d" % s][QUADS * h:QUADS * h + QUADS, t:4 * HALF:4],
-                    T["rd%d" % (s // 2)][lo:lo + QUADS, t * GW + h * HALF:t * GW + (h + 1) * HALF])
-        return (T["xt%d" % s][QUADS * h:QUADS * h + QUADS, 4 * XW * h + t:4 * XW * (h + 1):4],
-                T["rx%d" % (s // 2)][lo:lo + QUADS, t * XW:(t + 1) * XW])
+            b, c = (T["rd%d" % s], u * GW) if s < 2 else (T["rj%d" % s], u * JW + XW)
+            return T["gt%d" % s][to, t:4 * HALF:4], b[lo, c + h * HALF:c + (h + 1) * HALF]
+        b, c = (T.rx, (2 * s + u) * XW) if s < 2 else (T["rj%d" % s], u * JW)
+        return T["xt%d" % s][to, 4 * XW * h + t:4 * XW * (h + 1):4], b[lo, c:c + XW]
 
-    def copies(kind, k, t):
-        name = ("d%d_%d" if kind == "g" else "x%d_%d") % (k, t)
+    count = {}
+
+    def vcopy(kind, s, u, i, h):
+        to, of = views(kind, s, u, i, h)
+        name = "v%s%d" % (kind, s)
+        count[name] = count.get(name, 0) + 1
+        v.tensor_copy(to, of).then_inc(sem[name], 1)
+
+    def acopy(kind, s, u, i, h):
+        to, of = views(kind, s, u, i, h)
+        name = "s%s%d" % (kind, s)
+        count[name] = count.get(name, 0) + 1
+        a.activation(to, of, ActivationFunctionType.Copy).then_inc(sem[name], 1)
+
+    def copies(kind, s, u):
+        name = "%s%d_%d" % (kind, s, u)
         v.wait_ge(sem[name], 16)
         a.wait_ge(sem[name], 16)
-        o, i = views(kind, 2 * k + 1, 1, t)
-        a.activation(o, i, ActivationFunctionType.Copy).then_inc(sem["s%s%d" % (kind, k)], 1)
-        for s, h in ((2 * k, 0), (2 * k, 1), (2 * k + 1, 0)):
-            o, i = views(kind, s, h, t)
-            v.tensor_copy(o, i).then_inc(sem["v%s%d" % (kind, k)], 1)
+        if s >= 2:
+            acopy("x", s, u, 1, 0)
+            acopy("x", s, u, 1, 1)
+            vcopy("x", s, u, 0, 0)
+            vcopy("x", s, u, 0, 1)
+        acopy(kind, s, u, 1, 1)
+        vcopy(kind, s, u, 0, 0)
+        vcopy(kind, s, u, 0, 1)
+        vcopy(kind, s, u, 1, 0)
 
-    def quant(kind, k):
-        v.wait_ge(sem["v%s%d" % (kind, k)], 12)
+    def quant(kind, s):
         if kind == "x":
-            v.wait_ge(sem["zx%d" % k], 4)
-        for s in (2 * k, 2 * k + 1):
-            if s % 2:
-                v.wait_ge(sem["s%s%d" % (kind, k)], 4)
-            lo, hi = (0, HALF) if kind == "g" else (HALF, COLS)
-            tile = T["gt%d" % s] if kind == "g" else T["xt%d" % s]
-            v.quantize_mx(T["oc%d" % s][:, lo:hi], T["op%d" % s][:, lo:hi], tile[:]).then_inc(sem["q%s%d" % (kind, s)], 1)
+            v.wait_ge(sem["zx%d" % s], 2)
+        for q in "vs":
+            name = "%s%s%d" % (q, kind, s)
+            v.wait_ge(sem[name], count[name])
+        lo, hi = (0, HALF) if kind == "g" else (HALF, COLS)
+        tile = T["gt%d" % s] if kind == "g" else T["xt%d" % s]
+        v.quantize_mx(T["oc%d" % s][:, lo:hi], T["op%d" % s][:, lo:hi], tile[:]).then_inc(sem["q%s%d" % (kind, s)], 1)
 
-    def zeros_x(k):
-        for s in (2 * k, 2 * k + 1):
-            v.memset(T["xt%d" % s][QUADS:128, 0:4 * XW], 0.0).then_inc(sem["zx%d" % k], 1)
-            v.memset(T["xt%d" % s][0:QUADS, 4 * XW:8 * XW], 0.0).then_inc(sem["zx%d" % k], 1)
+    def zeros_x(s):
+        v.memset(T["xt%d" % s][QUADS:128, 0:4 * XW], 0.0).then_inc(sem["zx%d" % s], 1)
+        v.memset(T["xt%d" % s][0:QUADS, 4 * XW:8 * XW], 0.0).then_inc(sem["zx%d" % s], 1)
 
-    v.memset(T.rd0[:, 0:GW], 0.0).then_inc(sem.m0a, 1)
-    v.memset(T.rd0[:, GW:4 * GW], 0.0).then_inc(sem.m0b, 1)
-    v.memset(T.rx0[:], 0.0).then_inc(sem.m0b, 1)
+    v.memset(T.rd0[:, 0:GW], 0.0).then_inc(sem.ma, 1)
+    v.memset(T.rd0[:, GW:2 * GW], 0.0).then_inc(sem.mb, 1)
+    v.memset(T.rd1[:], 0.0).then_inc(sem.mb, 1)
+    v.memset(T.rx[:], 0.0).then_inc(sem.mx, 1)
     zeros_x(0)
-    copies("g", 0, 0)
-    v.memset(T.rd1[:, 0:2 * GW], 0.0).then_inc(sem.m1, 1)
-    copies("g", 0, 1)
-    v.memset(T.rd1[:, 2 * GW:4 * GW], 0.0).then_inc(sem.m1, 1)
-    copies("g", 0, 2)
-    v.memset(T.rx1[:], 0.0).then_inc(sem.m1, 1)
-    copies("g", 0, 3)
-    quant("g", 0)
     zeros_x(1)
-    for t in range(4):
-        copies("x", 0, t)
-    quant("x", 0)
-    for t in range(4):
-        copies("g", 1, t)
+    copies("g", 0, 0)
+    v.memset(T.rj2[:], 0.0).then_inc(sem.m2, 1)
+    copies("g", 0, 1)
+    quant("g", 0)
+    copies("g", 1, 0)
+    copies("g", 1, 1)
     quant("g", 1)
-    for t in range(4):
-        copies("x", 1, t)
-    quant("x", 1)
+    v.memset(T.rj3[:], 0.0).then_inc(sem.m3, 1)
+    zeros_x(2)
+    zeros_x(3)
+    for s in (0, 1):
+        copies("x", s, 0)
+        copies("x", s, 1)
+        quant("x", s)
+    for s in (2, 3):
+        copies("g", s, 0)
+        copies("g", s, 1)
+        quant("x", s)
+        quant("g", s)
 
     pe = g.tensor
-    order = [off[0], off[1], r, near]
+    order = [off[0], off[1], near, r]
     for j, s in enumerate(order):
         if s == r:
-            pe.wait_ge(sem.qg3, 1)
             pe.wait_ge(sem.qx3, 1)
+            pe.wait_ge(sem.qg3, 1)
             c, p = T.oc3, T.op3
         else:
-            pe.wait_ge(sem["arr%d" % s], 4 * len(near_eng) if s == near else 3 * half)
+            pe.wait_ge(sem["arr%d" % s], len(near_eng) + len(far_eng) if s == near else 3 * half)
             c, p = T["ic%d" % s], T["ip%d" % s]
         for h in range(2):
             w = slice(HALF + XW * h, HALF + XW * (h + 1))

@@ -6,19 +6,19 @@ JW = XW + GW
 HALF = GW // 2
 QUADS = 64
 COLS = HALF + 2 * XW
+MID = COLS // 2
 
 SCRATCH = {
     "tab": ("dram", [TOK, JW], "bfloat16"),
     "idx": ("sbuf", [128, 16], "int32"),
-    "rx": ("sbuf", [128, 4 * XW], "bfloat16"),
+    "rx0": ("sbuf", [128, 2 * XW], "bfloat16"),
     "rd0": ("sbuf", [128, 2 * GW], "bfloat16"),
-    "rd1": ("sbuf", [128, 2 * GW], "bfloat16"),
-    "rj2": ("sbuf", [128, 2 * JW], "bfloat16"),
-    "rj3": ("sbuf", [128, 2 * JW], "bfloat16"),
     "ys": ("sbuf", [128, GW], "float32"),
     "acc": ("psum", [128, GW], "float32"),
 }
 for _s in range(4):
+    if _s:
+        SCRATCH["rj%d" % _s] = ("sbuf", [128, 2 * JW], "bfloat16")
     SCRATCH["gt%d" % _s] = ("sbuf", [128, 4 * HALF], "bfloat16")
     SCRATCH["xt%d" % _s] = ("sbuf", [128, 8 * XW], "bfloat16")
     SCRATCH["oc%d" % _s] = ("sbuf", [128, COLS], "float8_e4m3fn_x4")
@@ -26,13 +26,12 @@ for _s in range(4):
     SCRATCH["ic%d" % _s] = ("sbuf", [128, COLS], "float8_e4m3fn_x4")
     SCRATCH["ip%d" % _s] = ("sbuf", [128, COLS], "uint8")
 
-SEMAPHORES = ["idx", "tab", "ma", "mb", "mx", "m2", "m3", "sent", "mm0", "mm1", "ev0", "ev1", "st0", "st1"]
+SEMAPHORES = ["idx", "ta", "tb", "tc", "td", "tx", "ma", "mb", "mx", "m1", "m2", "m3", "sent",
+              "mm0", "mm1", "ev0", "ev1", "st0", "st1", "x0_0", "x0_1"]
 for _s in range(4):
     SEMAPHORES += ["g%d_0" % _s, "g%d_1" % _s, "zx%d" % _s]
     SEMAPHORES += ["sg%d" % _s, "sx%d" % _s, "vg%d" % _s, "vx%d" % _s]
     SEMAPHORES += ["qg%d" % _s, "qx%d" % _s, "arr%d" % _s]
-for _s in range(2):
-    SEMAPHORES += ["x%d_0" % _s, "x%d_1" % _s]
 
 
 def bits(engines):
@@ -46,42 +45,46 @@ def rank_program(g, core, T, topo):
     cores = T.cores
     n = len(cores)
     sem = T.sem
-    off = [e for e in range(n) if topo.chip(cores[e]) != topo.chip(core)]
-    near = [e for e in range(n) if e != r and topo.chip(cores[e]) == topo.chip(core)][0]
-    slot = [off[0], off[1], near, r]
 
-    far_eng = topo.engines(core, cores[off[0]])
-    half = len(far_eng) // 2
+    def here(s):
+        return [e for e in range(n) if topo.chip(cores[e]) == topo.chip(cores[s])]
+
+    def far_order(s):
+        off = [e for e in range(n) if e not in here(s)]
+        return off if here(s)[0] == s else off[::-1]
+
+    far = far_order(r)
+    near = [e for e in here(r) if e != r][0]
+    slot = far + [near, r]
+    early = [s for s in far if far_order(s)[0] == r][0]
+    late = [s for s in far if s != early][0]
+
+    far_eng = topo.engines(core, cores[far[0]])
     near_eng = [e for e in topo.engines(core, cores[near]) if e not in far_eng]
 
     g.sync.dma_start(T.idx[0:QUADS, 0:15], T.pick[0:QUADS, 0:15]).then_inc(sem.idx, 16)
     g.scalar.dma_start(T.idx[QUADS:128, 0:15], T.pick[0:QUADS, 1:16]).then_inc(sem.idx, 16)
 
-    tabs = [0]
+    def tab_dy(j, name):
+        g.sync.dma_start(T.tab[128 * j:128 * j + 128, XW:JW], T.dy[128 * j:128 * j + 128, :]).then_inc(sem[name], 16)
 
-    def tab(kind, lo, hi):
-        to, of = (T.tab[lo:hi, XW:JW], T.dy[lo:hi, :]) if kind == "g" else (T.tab[lo:hi, 0:XW], T.x[lo:hi, :])
-        g.sync.dma_start(to, of).then_inc(sem.tab, 16)
-        tabs[0] += 16
-
-    for j in range(3):
-        tab("g", 128 * j, 128 * j + 128)
-    g.sync.wait_ge(sem.g0_0, 16)
-    tab("g", 384, 512)
-    g.sync.wait_ge(sem.g0_1, 16)
-    tab("x", 0, 512)
-    g.sync.wait_ge(sem.g1_0, 16)
-    tab("x", 512, 1024)
-    g.sync.wait_ge(sem.g1_1, 16)
-    for j in range(4, 8):
-        tab("g", 128 * j, 128 * j + 128)
+    g.dma_start(T.tab[:, 0:XW], T.x[:, :]).then_inc(sem.tx, 16)
+    for j in (0, 1, 2):
+        tab_dy(j, "ta")
+    tab_dy(3, "tb")
+    g.sync.wait_ge(sem.ta, 48)
+    tab_dy(4, "tc")
+    tab_dy(5, "tc")
+    g.sync.wait_ge(sem.tb, 16)
+    tab_dy(6, "td")
+    tab_dy(7, "td")
 
     def gather(kind, s, u):
         c = 4 * slot[s] + 2 * u
         if kind == "x":
-            land, table = T.rx[:, (2 * s + u) * XW:(2 * s + u + 1) * XW], T.x[:]
-        elif s < 2:
-            land, table = T["rd%d" % s][:, u * GW:(u + 1) * GW], T.dy[:]
+            land, table = T.rx0[:, u * XW:(u + 1) * XW], T.x[:]
+        elif s == 0:
+            land, table = T.rd0[:, u * GW:(u + 1) * GW], T.dy[:]
         else:
             land, table = T["rj%d" % s][:, u * JW:(u + 1) * JW], T.tab[:]
         g.indirect_dma_start(land, None, table, IndirectOffsetOnAxis(ap=T.idx[:, c:c + 1], axis=0),
@@ -93,9 +96,9 @@ def rank_program(g, core, T, topo):
 
     sent = [0]
 
-    def send(parts, codes, lo, hi):
+    def send(s, parts):
         tr = []
-        for s, engines in parts:
+        for codes, engines, lo, hi in parts:
             src, dst = ("oc%d" % s, "ic%d" % r) if codes else ("op%d" % s, "ip%d" % r)
             src, dst = T[src][:, lo:hi], T[dst][:, lo:hi]
             if codes:
@@ -105,37 +108,41 @@ def rank_program(g, core, T, topo):
                                         remote_sem=sem["arr%d" % r], src=src, dst=dst))
         g.remote_dma_fused(tr, local_sem=sem.sent)
 
-    far = [(0, far_eng[:half]), (1, far_eng[half:])]
     g.wait_ge(sem.idx, 32)
     g.wait_ge(sem.ma, 1)
     gather("g", 0, 0)
-    g.wait_ge(sem.mb, 2)
+    g.wait_ge(sem.mb, 1)
     gather("g", 0, 1)
-    gather("g", 1, 0)
-    gather("g", 1, 1)
     g.wait_ge(sem.mx, 1)
     gather("x", 0, 0)
     gather("x", 0, 1)
-    gather("x", 1, 0)
     g.wait_ge(sem.qg0, 1)
-    g.wait_ge(sem.qg1, 1)
-    send(far, True, 0, HALF)
-    gather("x", 1, 1)
+    send(0, [(True, far_eng, 0, HALF)])
+    g.wait_ge(sem.m1, 1)
+    g.wait_ge(sem.tx, 16)
+    g.wait_ge(sem.ta, 48)
+    g.wait_ge(sem.tb, 16)
+    g.wait_ge(sem.tc, 32)
+    g.wait_ge(sem.td, 32)
+    gather("g", 1, 0)
+    gather("g", 1, 1)
+    g.wait_ge(sem.qx0, 1)
+    send(0, [(True, far_eng, HALF, COLS)])
+    send(0, [(False, far_eng, 0, COLS)])
     g.wait_ge(sem.m2, 1)
-    g.wait_ge(sem.tab, tabs[0])
     gather("g", 2, 0)
     gather("g", 2, 1)
-    g.wait_ge(sem.qx0, 1)
-    g.wait_ge(sem.qx1, 1)
-    send(far, True, HALF, COLS)
-    send(far, False, 0, COLS)
     g.wait_ge(sem.m3, 1)
     gather("g", 3, 0)
+    g.wait_ge(sem.qx1, 1)
+    g.wait_ge(sem.qg1, 1)
+    send(1, [(True, far_eng, 0, COLS)])
+    send(1, [(False, far_eng, 0, COLS)])
     gather("g", 3, 1)
     g.wait_ge(sem.qx2, 1)
     g.wait_ge(sem.qg2, 1)
-    send([(2, near_eng)], True, 0, COLS)
-    send([(2, far_eng)], False, 0, COLS)
+    send(2, [(True, near_eng, 0, MID), (True, far_eng, MID, COLS)])
+    send(2, [(False, near_eng, 0, COLS)])
     g.wait_ge(sem.sent, sent[0])
 
     v, a = g.vector, g.scalar
@@ -144,9 +151,9 @@ def rank_program(g, core, T, topo):
         t = 2 * u + i
         lo, to = slice(QUADS * i, QUADS * (i + 1)), slice(QUADS * h, QUADS * (h + 1))
         if kind == "g":
-            b, c = (T["rd%d" % s], u * GW) if s < 2 else (T["rj%d" % s], u * JW + XW)
+            b, c = (T.rd0, u * GW) if s == 0 else (T["rj%d" % s], u * JW + XW)
             return T["gt%d" % s][to, t:4 * HALF:4], b[lo, c + h * HALF:c + (h + 1) * HALF]
-        b, c = (T.rx, (2 * s + u) * XW) if s < 2 else (T["rj%d" % s], u * JW)
+        b, c = (T.rx0, u * XW) if s == 0 else (T["rj%d" % s], u * JW)
         return T["xt%d" % s][to, 4 * XW * h + t:4 * XW * (h + 1):4], b[lo, c:c + XW]
 
     count = {}
@@ -167,7 +174,7 @@ def rank_program(g, core, T, topo):
         name = "%s%d_%d" % (kind, s, u)
         v.wait_ge(sem[name], 16)
         a.wait_ge(sem[name], 16)
-        if s >= 2:
+        if s:
             acopy("x", s, u, 1, 0)
             acopy("x", s, u, 1, 1)
             vcopy("x", s, u, 0, 0)
@@ -193,39 +200,36 @@ def rank_program(g, core, T, topo):
 
     v.memset(T.rd0[:, 0:GW], 0.0).then_inc(sem.ma, 1)
     v.memset(T.rd0[:, GW:2 * GW], 0.0).then_inc(sem.mb, 1)
-    v.memset(T.rd1[:], 0.0).then_inc(sem.mb, 1)
-    v.memset(T.rx[:], 0.0).then_inc(sem.mx, 1)
+    v.memset(T.rx0[:], 0.0).then_inc(sem.mx, 1)
+    v.memset(T.rj1[:], 0.0).then_inc(sem.m1, 1)
     zeros_x(0)
-    zeros_x(1)
     copies("g", 0, 0)
-    v.memset(T.rj2[:], 0.0).then_inc(sem.m2, 1)
+    zeros_x(1)
     copies("g", 0, 1)
     quant("g", 0)
-    copies("g", 1, 0)
-    copies("g", 1, 1)
-    quant("g", 1)
+    v.memset(T.rj2[:], 0.0).then_inc(sem.m2, 1)
+    copies("x", 0, 0)
+    copies("x", 0, 1)
+    quant("x", 0)
     v.memset(T.rj3[:], 0.0).then_inc(sem.m3, 1)
     zeros_x(2)
     zeros_x(3)
-    for s in (0, 1):
-        copies("x", s, 0)
-        copies("x", s, 1)
-        quant("x", s)
-    for s in (2, 3):
+    for s in (1, 2, 3):
         copies("g", s, 0)
         copies("g", s, 1)
         quant("x", s)
         quant("g", s)
 
     pe = g.tensor
-    order = [off[0], off[1], near, r]
+    order = [early, r, near, late]
+    incs = {early: 3 * len(far_eng), late: 2 * len(far_eng), near: 2 * len(near_eng) + len(far_eng)}
     for j, s in enumerate(order):
         if s == r:
             pe.wait_ge(sem.qx3, 1)
             pe.wait_ge(sem.qg3, 1)
             c, p = T.oc3, T.op3
         else:
-            pe.wait_ge(sem["arr%d" % s], len(near_eng) + len(far_eng) if s == near else 3 * half)
+            pe.wait_ge(sem["arr%d" % s], incs[s])
             c, p = T["ic%d" % s], T["ip%d" % s]
         for h in range(2):
             w = slice(HALF + XW * h, HALF + XW * (h + 1))

from concourse.bass import DstId, RemoteDMATransfer, IndirectOffsetOnAxis
from concourse.mybir import dt, ActivationFunctionType

TOK, XW, GW = 1024, 128, 1024
JW = XW + GW
HALF = GW // 2
QUADS = 64
COLS = HALF + 2 * XW
MID = COLS // 2

SCRATCH = {
    "tab": ("dram", [TOK, JW], "bfloat16"),
    "idx": ("sbuf", [128, 16], "int32"),
    "rx0": ("sbuf", [128, 2 * XW], "bfloat16"),
    "rd0": ("sbuf", [128, 2 * GW], "bfloat16"),
    "ys": ("sbuf", [128, GW], "float32"),
    "acc": ("psum", [128, GW], "float32"),
}
for _s in range(4):
    if _s:
        SCRATCH["rj%d" % _s] = ("sbuf", [128, 2 * JW], "bfloat16")
    SCRATCH["gt%d" % _s] = ("sbuf", [128, 4 * HALF], "bfloat16")
    SCRATCH["xt%d" % _s] = ("sbuf", [128, 8 * XW], "bfloat16")
    SCRATCH["oc%d" % _s] = ("sbuf", [128, COLS], "float8_e4m3fn_x4")
    SCRATCH["op%d" % _s] = ("sbuf", [128, COLS], "uint8")
    SCRATCH["ic%d" % _s] = ("sbuf", [128, COLS], "float8_e4m3fn_x4")
    SCRATCH["ip%d" % _s] = ("sbuf", [128, COLS], "uint8")

SEMAPHORES = ["idx", "ta", "tb", "tc", "td", "tx", "ma", "mb", "mx", "m1", "m2", "m3", "sent",
              "mm0", "mm1", "ev0", "ev1", "st0", "st1", "x0_0", "x0_1"]
for _s in range(4):
    SEMAPHORES += ["g%d_0" % _s, "g%d_1" % _s, "zx%d" % _s]
    SEMAPHORES += ["sg%d" % _s, "sx%d" % _s, "vg%d" % _s, "vx%d" % _s]
    SEMAPHORES += ["qg%d" % _s, "qx%d" % _s, "arr%d" % _s]


def bits(engines):
    return sum(1 << e for e in engines)


def rank_program(g, core, T, topo):
    r = T.rank_of(core)
    if r is None:
        return
    cores = T.cores
    n = len(cores)
    sem = T.sem

    def here(s):
        return [e for e in range(n) if topo.chip(cores[e]) == topo.chip(cores[s])]

    def far_order(s):
        off = [e for e in range(n) if e not in here(s)]
        return off if here(s)[0] == s else off[::-1]

    far = far_order(r)
    near = [e for e in here(r) if e != r][0]
    slot = far + [near, r]
    early = [s for s in far if far_order(s)[0] == r][0]
    late = [s for s in far if s != early][0]

    far_eng = topo.engines(core, cores[far[0]])
    near_eng = [e for e in topo.engines(core, cores[near]) if e not in far_eng]

    g.sync.dma_start(T.idx[0:QUADS, 0:15], T.pick[0:QUADS, 0:15]).then_inc(sem.idx, 16)
    g.scalar.dma_start(T.idx[QUADS:128, 0:15], T.pick[0:QUADS, 1:16]).then_inc(sem.idx, 16)

    def tab_dy(j, name):
        g.sync.dma_start(T.tab[128 * j:128 * j + 128, XW:JW], T.dy[128 * j:128 * j + 128, :]).then_inc(sem[name], 16)

    g.dma_start(T.tab[:, 0:XW], T.x[:, :]).then_inc(sem.tx, 16)
    for j in (0, 1, 2):
        tab_dy(j, "ta")
    tab_dy(3, "tb")
    g.sync.wait_ge(sem.ta, 48)
    tab_dy(4, "tc")
    tab_dy(5, "tc")
    g.sync.wait_ge(sem.tb, 16)
    tab_dy(6, "td")
    tab_dy(7, "td")

    def gather(kind, s, u):
        c = 4 * slot[s] + 2 * u
        if kind == "x":
            land, table = T.rx0[:, u * XW:(u + 1) * XW], T.x[:]
        elif s == 0:
            land, table = T.rd0[:, u * GW:(u + 1) * GW], T.dy[:]
        else:
            land, table = T["rj%d" % s][:, u * JW:(u + 1) * JW], T.tab[:]
        g.indirect_dma_start(land, None, table, IndirectOffsetOnAxis(ap=T.idx[:, c:c + 1], axis=0),
                             bounds_check=TOK - 1, oob_is_err=False).then_inc(sem["%s%d_%d" % (kind, s, u)], 16)

    def dst_id(e):
        rid, pid, _ = topo.addr(cores[e])
        return DstId(rid=rid, pnc=pid)

    sent = [0]

    def send(s, parts):
        tr = []
        for codes, engines, lo, hi in parts:
            src, dst = ("oc%d" % s, "ic%d" % r) if codes else ("op%d" % s, "ip%d" % r)
            src, dst = T[src][:, lo:hi], T[dst][:, lo:hi]
            if codes:
                src, dst = src.bitcast(dt.uint8), dst.bitcast(dt.uint8)
            sent[0] += len(engines)
            tr.append(RemoteDMATransfer(dst_ids=[dst_id(slot[s])], dma_engine_mask=bits(engines),
                                        remote_sem=sem["arr%d" % r], src=src, dst=dst))
        g.remote_dma_fused(tr, local_sem=sem.sent)

    g.wait_ge(sem.idx, 32)
    g.wait_ge(sem.ma, 1)
    gather("g", 0, 0)
    g.wait_ge(sem.mb, 1)
    gather("g", 0, 1)
    g.wait_ge(sem.mx, 1)
    gather("x", 0, 0)
    gather("x", 0, 1)
    g.wait_ge(sem.qg0, 1)
    send(0, [(True, far_eng, 0, HALF)])
    g.wait_ge(sem.m1, 1)
    g.wait_ge(sem.tx, 16)
    g.wait_ge(sem.ta, 48)
    g.wait_ge(sem.tb, 16)
    g.wait_ge(sem.tc, 32)
    g.wait_ge(sem.td, 32)
    gather("g", 1, 0)
    gather("g", 1, 1)
    g.wait_ge(sem.qx0, 1)
    send(0, [(True, far_eng, HALF, COLS)])
    send(0, [(False, far_eng, 0, COLS)])
    g.wait_ge(sem.m2, 1)
    gather("g", 2, 0)
    gather("g", 2, 1)
    g.wait_ge(sem.m3, 1)
    gather("g", 3, 0)
    g.wait_ge(sem.qx1, 1)
    g.wait_ge(sem.qg1, 1)
    send(1, [(True, far_eng, 0, COLS)])
    send(1, [(False, far_eng, 0, COLS)])
    gather("g", 3, 1)
    g.wait_ge(sem.qx2, 1)
    g.wait_ge(sem.qg2, 1)
    send(2, [(True, near_eng, 0, MID), (True, far_eng, MID, COLS)])
    send(2, [(False, near_eng, 0, COLS)])
    g.wait_ge(sem.sent, sent[0])

    v, a = g.vector, g.scalar

    def views(kind, s, u, i, h):
        t = 2 * u + i
        lo, to = slice(QUADS * i, QUADS * (i + 1)), slice(QUADS * h, QUADS * (h + 1))
        if kind == "g":
            b, c = (T.rd0, u * GW) if s == 0 else (T["rj%d" % s], u * JW + XW)
            return T["gt%d" % s][to, t:4 * HALF:4], b[lo, c + h * HALF:c + (h + 1) * HALF]
        b, c = (T.rx0, u * XW) if s == 0 else (T["rj%d" % s], u * JW)
        return T["xt%d" % s][to, 4 * XW * h + t:4 * XW * (h + 1):4], b[lo, c:c + XW]

    count = {}

    def vcopy(kind, s, u, i, h):
        to, of = views(kind, s, u, i, h)
        name = "v%s%d" % (kind, s)
        count[name] = count.get(name, 0) + 1
        v.tensor_copy(to, of).then_inc(sem[name], 1)

    def acopy(kind, s, u, i, h):
        to, of = views(kind, s, u, i, h)
        name = "s%s%d" % (kind, s)
        count[name] = count.get(name, 0) + 1
        a.activation(to, of, ActivationFunctionType.Copy).then_inc(sem[name], 1)

    def copies(kind, s, u):
        name = "%s%d_%d" % (kind, s, u)
        v.wait_ge(sem[name], 16)
        a.wait_ge(sem[name], 16)
        if s:
            acopy("x", s, u, 1, 0)
            acopy("x", s, u, 1, 1)
            vcopy("x", s, u, 0, 0)
            vcopy("x", s, u, 0, 1)
        acopy(kind, s, u, 1, 1)
        vcopy(kind, s, u, 0, 0)
        vcopy(kind, s, u, 0, 1)
        vcopy(kind, s, u, 1, 0)

    def quant(kind, s):
        if kind == "x":
            v.wait_ge(sem["zx%d" % s], 2)
        for q in "vs":
            name = "%s%s%d" % (q, kind, s)
            v.wait_ge(sem[name], count[name])
        lo, hi = (0, HALF) if kind == "g" else (HALF, COLS)
        tile = T["gt%d" % s] if kind == "g" else T["xt%d" % s]
        v.quantize_mx(T["oc%d" % s][:, lo:hi], T["op%d" % s][:, lo:hi], tile[:]).then_inc(sem["q%s%d" % (kind, s)], 1)

    def zeros_x(s):
        v.memset(T["xt%d" % s][QUADS:128, 0:4 * XW], 0.0).then_inc(sem["zx%d" % s], 1)
        v.memset(T["xt%d" % s][0:QUADS, 4 * XW:8 * XW], 0.0).then_inc(sem["zx%d" % s], 1)

    v.memset(T.rd0[:, 0:GW], 0.0).then_inc(sem.ma, 1)
    v.memset(T.rd0[:, GW:2 * GW], 0.0).then_inc(sem.mb, 1)
    v.memset(T.rx0[:], 0.0).then_inc(sem.mx, 1)
    v.memset(T.rj1[:], 0.0).then_inc(sem.m1, 1)
    zeros_x(0)
    copies("g", 0, 0)
    zeros_x(1)
    copies("g", 0, 1)
    quant("g", 0)
    v.memset(T.rj2[:], 0.0).then_inc(sem.m2, 1)
    copies("x", 0, 0)
    copies("x", 0, 1)
    quant("x", 0)
    v.memset(T.rj3[:], 0.0).then_inc(sem.m3, 1)
    zeros_x(2)
    zeros_x(3)
    for s in (1, 2, 3):
        copies("g", s, 0)
        copies("g", s, 1)
        quant("x", s)
        quant("g", s)

    pe = g.tensor
    order = [early, r, near, late]
    incs = {early: 3 * len(far_eng), late: 2 * len(far_eng), near: 2 * len(near_eng) + len(far_eng)}
    for j, s in enumerate(order):
        if s == r:
            pe.wait_ge(sem.qx3, 1)
            pe.wait_ge(sem.qg3, 1)
            c, p = T.oc3, T.op3
        else:
            pe.wait_ge(sem["arr%d" % s], incs[s])
            c, p = T["ic%d" % s], T["ip%d" % s]
        for h in range(2):
            w = slice(HALF + XW * h, HALF + XW * (h + 1))
            m = pe.matmul_mx(T.acc[:, HALF * h:HALF * (h + 1)], c[:, w], p[:, w], c[:, 0:HALF], p[:, 0:HALF],
                             j == 0, j == n - 1)
            if j == n - 1:
                m.then_inc(sem["mm%d" % h], 1)

    v.wait_ge(sem.mm0, 1)
    v.tensor_copy(T.ys[:, 0:HALF], T.acc[:, 0:HALF]).then_inc(sem.ev0, 1)
    g.sync.wait_ge(sem.ev0, 1)
    g.sync.dma_start(T.y[:, 0:HALF], T.ys[:, 0:HALF]).then_inc(sem.st0, 16)
    g.sync.wait_ge(sem.st0, 16)
    a.wait_ge(sem.mm1, 1)
    a.activation(T.ys[:, HALF:GW], T.acc[:, HALF:GW], ActivationFunctionType.Copy).then_inc(sem.ev1, 1)
    a.wait_ge(sem.ev1, 1)
    a.dma_start(T.y[:, HALF:GW], T.ys[:, HALF:GW]).then_inc(sem.st1, 16)
    a.wait_ge(sem.st1, 16)
